import numpy as np
import ml_dtypes


def mxq(x, axis, fmt="e4m3"):
    dtype, down = {"e4m3": (ml_dtypes.float8_e4m3fn, 7), "e5m2": (ml_dtypes.float8_e5m2, 14)}[fmt]
    v = np.moveaxis(np.asarray(x, np.float32).astype(ml_dtypes.bfloat16).astype(np.float64), axis, -1)
    blocks = v.reshape(v.shape[:-1] + (-1, 32))
    amax = np.abs(blocks).max(-1, keepdims=True)
    byte = np.maximum(np.where(amax > 0, np.frexp(amax)[1] - 1 + 127, 0) - down, 1)
    scale = np.exp2(byte - 127.0)
    codes = (blocks / scale).astype(np.float32).astype(dtype).astype(np.float64)
    return np.moveaxis((codes * scale).reshape(v.shape), -1, axis)


WIDE = False


def mx_kscale(k):
    if not WIDE:
        return np.ones(k)
    levels = np.array([10, -10, 5, -5, 0])
    if k % 512:
        return np.exp2(np.random.permutation(np.resize(levels, k // 32))).repeat(32)
    a = np.empty((k // 512, 16))
    for p in range(k // 512):
        a[p, :8] = np.random.permutation(np.resize(levels, 8))
        for g in range(8):
            far = levels[np.abs(levels - a[p, g]) >= 10]
            a[p, g + 8] = far[np.random.randint(len(far))]
    return np.exp2(a.ravel()).repeat(32)


def f64(x):
    return np.asarray(x).astype(np.float64)


def striped(idx):
    return np.tile(idx.reshape(-1, 16).T, (8, 1)).astype(np.uint16)


def unstriped(offs):
    return offs[:16].T.reshape(-1).astype(np.int64)


def striped8(idx):
    return np.concatenate([x.reshape(-1, 16).T for x in idx]).astype(np.uint16)


def runs(offs, k):
    lists = np.stack([offs[16 * r : 16 * r + 16].T.reshape(-1) for r in range(8)]).astype(np.int64)
    return lists[np.arange(k) % 512 // 64]


def pack_weight(w):
    k, n = w.shape
    w = f64(np.asarray(w, np.float32).astype(ml_dtypes.bfloat16)).reshape(k // 32, 32, n)
    amax = np.abs(w).max(1)
    byte = np.clip(np.where(amax > 0, np.frexp(amax)[1] - 1 + 127 - 7, 1), 1, 254)
    scaled = (w * np.exp2(127.0 - byte)[:, None, :]).reshape(k, n).astype(np.float32)
    words = np.ascontiguousarray(scaled.reshape(k // 512, 128, 4, n).transpose(0, 1, 3, 2)).astype(ml_dtypes.float8_e4m3fn).view(np.uint8)
    return words, np.ascontiguousarray(byte.astype(np.uint8).reshape(k // 512, 16, n))


def unpack_weight(words, scales):
    g, p, n, _ = words.shape
    vals = np.ascontiguousarray(words).view(ml_dtypes.float8_e4m3fn).astype(np.float64) * np.repeat(np.exp2(scales.astype(np.float64) - 127.0), 8, axis=1)[..., None]
    return vals.transpose(0, 1, 3, 2).reshape(g * 512, n)


K, T, S, N, G, H, W = 512, 1024, 256, 512, 2048, 512, 128


def setup_inputs():
    n = np.random.standard_normal
    s = mx_kscale(K)[:, None]
    u = mx_kscale(K)
    packed_xT = pack_weight(n((K, T)) * s)
    packed_dT = pack_weight(n((K, G)) / s)
    perm = np.random.permutation(S)
    perm2 = np.random.permutation(S)
    return {
        "x_words": packed_xT[0],
        "x_scales": packed_xT[1],
        "d_words": packed_dT[0],
        "d_scales": packed_dT[1],
        "gn": (np.random.uniform(0.5, 1.5, (H, 1)) * u[:, None]).astype(np.float32),
        "w1": (n((H, N)) / np.sqrt(H) / u[:, None]).astype(np.float32),
        "offs": striped8(np.random.randint(0, T, (8, S))),
        "k1": striped8(np.random.randint(0, G, (8, H))),
        "hz": striped8(np.random.randint(0, T, (8, S))),
        "k2": striped8(np.random.randint(0, G, (8, H))),
        "n1": striped(np.random.permutation(S)),
        "n2": striped(np.random.permutation(S)),
        "n3": striped(perm[:W]),
        "n4": striped(perm[W:]),
        "n5": striped(perm2[:W]),
        "n6": striped(perm2[W:]),
        "n7": striped(np.random.permutation(S)),
    }


def reference(x_words, x_scales, d_words, d_scales, gn, w1, offs, k1, hz, k2, n1, n2, n3, n4, n5, n6, n7):
    d_k1 = unpack_weight(d_words, d_scales)[np.arange(K)[:, None], runs(k1, K)]
    xq = unpack_weight(x_words, x_scales)[np.arange(K)[:, None], runs(offs, K)]
    d_k2 = unpack_weight(d_words, d_scales)[np.arange(K)[:, None], runs(k2, K)]
    x_hz = unpack_weight(x_words, x_scales)[np.arange(K)[:, None], runs(hz, K)]
    h = 0.0625 * (d_k1.T @ xq + d_k2.T @ x_hz)
    st = np.maximum(h, h[:, unstriped(n1)])
    ds = np.zeros((H, S))
    ds[:, unstriped(n2)] = st
    z = f64(gn) * (ds - h)
    h2 = mxq(f64(w1), 0, "e4m3").T @ mxq(z, 0, "e4m3")
    pa = h2[:, unstriped(n3)]
    pb = h2[:, unstriped(n4)]
    rb = np.maximum(pa, pb)
    ra = pa + pb
    ua = np.zeros((N, S))
    ua[:, unstriped(n5)] = ra
    ub = ua.copy()
    ub[:, unstriped(n6)] = rb
    return ub - ub[:, unstriped(n7)]

@@ -1,0 +1,213 @@
+from contextlib import ExitStack
+
+import concourse.mybir as mybir
+
+K, T, S, N, G, H, W = 512, 1024, 256, 512, 2048, 512, 128
+FLOPS = 2 * (2 * K * H * S + H * N * S)
+
+F32 = mybir.dt.float32
+BF16 = mybir.dt.bfloat16
+I32 = mybir.dt.int32
+U32 = mybir.dt.uint32
+U16 = mybir.dt.uint16
+U8 = mybir.dt.uint8
+FP8X4 = mybir.dt.float8_e4m3fn_x4
+ALU = mybir.AluOpType
+COPY = mybir.ActivationFunctionType.Copy
+
+P = 128
+SLOTS = 4
+SPARE = 8
+SCATTER_COLS = 352
+
+
+def tile_picked_mhhznsendhopcphd_none_p_kernel(
+    tc, x_words, x_scales, d_words, d_scales, gn, w1, offs, k1, hz, k2, n1, n2, n3, n4, n5, n6, n7, out
+):
+    nc = tc.nc
+    with ExitStack() as ctx:
+        keep = ctx.enter_context(tc.tile_pool(name="keep", bufs=1))
+        psum = ctx.enter_context(tc.psum_pool(name="psum", bufs=1))
+
+        def load_list(name, src):
+            tile = keep.tile(list(src.shape), U16, name=name)
+            nc.sync.dma_start(tile[:], src)
+            return tile
+
+        d_bytes = keep.tile([P, G], U8, align_bytes=64)
+        x_bytes = keep.tile([P, T], U8, align_bytes=64)
+        d_tab = keep.tile([P, G], U32, align_bytes=64)
+        x_tab = keep.tile([P, T], U32, align_bytes=64)
+        offs_t = load_list("offs_t", offs)
+        nc.sync.dma_start(
+            x_bytes[:].bitcast(I32), x_scales[0].bitcast(I32).unsqueeze(1).to_broadcast([16, 8, T // 4])
+        )
+        hz_t = load_list("hz_t", hz)
+        nc.sync.dma_start(
+            d_bytes[:].bitcast(I32), d_scales[0].bitcast(I32).unsqueeze(1).to_broadcast([16, 8, G // 4])
+        )
+        k1_t = load_list("k1_t", k1)
+        k2_t = load_list("k2_t", k2)
+        nc.sync.dma_start(d_tab[:].bitcast(I32), d_words[0].rearrange("p c r -> p (c r)").bitcast(I32))
+        nc.sync.dma_start(x_tab[:].bitcast(I32), x_words[0].rearrange("p c r -> p (c r)").bitcast(I32))
+
+        n1_t = load_list("n1_t", n1)
+        n2_t = load_list("n2_t", n2)
+        n3_t = load_list("n3_t", n3)
+        n4_t = load_list("n4_t", n4)
+        n5_t = load_list("n5_t", n5)
+        n6_t = load_list("n6_t", n6)
+        n7_t = load_list("n7_t", n7)
+        gain = [keep.tile([P, 1], F32, name="gain%d" % t) for t in range(SLOTS)]
+        gn_rows = gn.rearrange("(b t q) o -> t b q o", t=SLOTS, q=8)
+        for t in range(SLOTS):
+            nc.sync.dma_start(gain[t][:], gn_rows[t])
+
+        planes = keep.tile([P, 2 * H + 2 * S], U8, align_bytes=64)
+        nc.vector.memset(planes[:].bitcast(I32), 0)
+        h_t = [keep.tile([P, S + SPARE], F32, name="h%d" % t) for t in range(SLOTS)]
+        ub_t = [keep.tile([P, S + SPARE], F32, name="ub%d" % t) for t in range(SLOTS)]
+        for tile in h_t + ub_t:
+            nc.vector.memset(tile[:, S:], 0.0)
+
+        picked_bytes = keep.tile([P, 2 * H + 2 * S], U8, align_bytes=64)
+        nc.vector.tensor_copy(picked_bytes[:, 2 * H : 2 * H + S], x_bytes[:].indirect(offs_t[:]))
+        nc.vector.tensor_copy(picked_bytes[:, 2 * H + S :], x_bytes[:].indirect(hz_t[:]))
+        nc.vector.tensor_copy(picked_bytes[:, 0:H], d_bytes[:].indirect(k1_t[:]))
+        nc.vector.tensor_copy(picked_bytes[:, H : 2 * H], d_bytes[:].indirect(k2_t[:]))
+        dealt_bytes = keep.tile([P, 2 * H + 2 * S], U8, tag="staging", align_bytes=64)
+        nc.vector.tensor_copy(dealt_bytes[:, 2 * H :].bitcast(I32), picked_bytes[:, 2 * H :].bitcast(I32))
+        nc.vector.tensor_copy(
+            dealt_bytes[:, : 2 * H].bitcast(I32).rearrange("p (l t b w) -> p l t b w", l=2, t=SLOTS, w=2),
+            picked_bytes[:, : 2 * H].bitcast(I32).rearrange("p (l b t w) -> p l t b w", l=2, t=SLOTS, w=2),
+        )
+        for a in range(4):
+            queue = nc.sync if a % 2 == 0 else nc.scalar
+            queue.dma_start(planes[a:P:32, :].bitcast(I32), dealt_bytes[8 * a : P : 32, :].bitcast(I32))
+
+        picked_d = keep.tile([P, 2 * H], U32, align_bytes=64)
+        picked_x = [keep.tile([P, S], U32, name="picked_x%d" % l, align_bytes=64) for l in range(2)]
+        dealt_d = keep.tile([P, 2 * H], U32, align_bytes=64)
+        deal_to = dealt_d[:].rearrange("p (l t b q) -> p l t b q", l=2, t=SLOTS, q=8)
+        deal_from = picked_d[:].rearrange("p (l b t q) -> p l t b q", l=2, t=SLOTS, q=8)
+
+        nc.vector.tensor_copy(picked_d[:, :H], d_tab[:].indirect(k1_t[:]))
+        nc.vector.tensor_copy(picked_d[:, H:], d_tab[:].indirect(k2_t[:]))
+        nc.vector.tensor_copy(picked_x[0][:], x_tab[:].indirect(offs_t[:]))
+        nc.vector.tensor_copy(deal_to[:, :, 0], deal_from[:, :, 0])
+        nc.vector.tensor_copy(picked_x[1][:], x_tab[:].indirect(hz_t[:]))
+        nc.vector.tensor_copy(deal_to[:, :, 1:], deal_from[:, :, 1:])
+
+        w_raw = keep.tile([P, SLOTS, N], F32, tag="staging", align_bytes=64)
+        w_rows = w1.rearrange("(b t q) n -> t b q n", t=SLOTS, q=8)
+        for t in range(SLOTS):
+            nc.sync.dma_start(w_raw[:, t, :], w_rows[t])
+
+        halves = [slice(0, S // 2), slice(S // 2, S)]
+        z_bf = keep.tile([P, S, SLOTS], BF16, align_bytes=64)
+        w_codes = keep.tile([P, N], U32, align_bytes=64)
+        w_scales = keep.tile([P, N], U8, align_bytes=64)
+
+        acc_h = [psum.tile([P, S], F32, name="acc_h%d" % t) for t in range(SLOTS)]
+        for t in range(SLOTS):
+            for l in range(2):
+                cols = slice(l * H + t * P, l * H + (t + 1) * P)
+                nc.tensor.matmul_mx(
+                    out=acc_h[t][:],
+                    lhsT=dealt_d[:, cols].bitcast(FP8X4),
+                    lhsT_scale=planes[:, cols],
+                    rhs=picked_x[l][:].bitcast(FP8X4),
+                    rhs_scale=planes[:, 2 * H + l * S : 2 * H + (l + 1) * S],
+                    start=(l == 0),
+                    stop=(l == 1),
+                )
+
+        nc.scalar.activation(h_t[0][:, :S], acc_h[0][:], COPY, scale=0.0625)
+        for t in range(1, SLOTS):
+            nc.vector.tensor_scalar(h_t[t][:, :S], acc_h[t][:], 0.0625, None, ALU.mult)
+        hopped = [keep.tile([P, S], F32, name="hopped%d" % t) for t in range(SLOTS)]
+        st = [keep.tile([P, S], F32, name="st%d" % t) for t in range(SLOTS)]
+        for t in range(SLOTS):
+            nc.scalar.activation(hopped[t][:], h_t[t][:].indirect(n1_t[:]), COPY)
+            nc.vector.tensor_tensor(st[t][:], h_t[t][:, :S], hopped[t][:], ALU.max)
+
+        for t in range(SLOTS):
+            ds = keep.tile([P, SCATTER_COLS], F32, name="ds%d" % t)
+            nc.scalar.activation(ds[:].indirect(n2_t[:]), st[t][:], COPY)
+            gained_h = keep.tile([P, S], F32, name="gained_h%d" % t)
+            nc.vector.tensor_scalar(gained_h[:], h_t[t][:, :S], gain[t][:], None, ALU.mult)
+            cols = slice(t * P, (t + 1) * P)
+            w_bf = keep.tile([P, P, SLOTS], BF16, name="w_bf%d" % t, align_bytes=64)
+            nc.vector.tensor_copy(
+                w_bf[:].rearrange("p (c i) t -> p c t i", i=4),
+                w_raw[:, :, cols].rearrange("p t (c i) -> p c t i", i=4),
+            )
+            nc.vector.quantize_mx(
+                out=w_codes[:, cols].bitcast(FP8X4),
+                scales=w_scales[:, cols],
+                in_=w_bf[:].rearrange("p c t -> p (c t)"),
+            )
+            for part in halves if t == SLOTS - 1 else [slice(0, S)]:
+                nc.vector.scalar_tensor_tensor(
+                    z_bf[:, part, t], ds[:, part], gain[t][:], gained_h[:, part], ALU.mult, ALU.subtract
+                )
+
+        z_codes = keep.tile([P, S], U32, align_bytes=64)
+        z_scales = keep.tile([P, S], U8, align_bytes=64)
+        for part in halves:
+            nc.vector.quantize_mx(
+                out=z_codes[:, part].bitcast(FP8X4),
+                scales=z_scales[:, part],
+                in_=z_bf[:, part, :].rearrange("p j t -> p (j t)"),
+            )
+
+        blocks = N // P
+        h2 = [keep.tile([P, S], F32, name="h2_%d" % m) for m in range(blocks)]
+
+        def product(m, part, bank):
+            cols = slice(m * P, (m + 1) * P)
+            acc = psum.tile([P, part.stop - part.start], F32, name=bank)
+            nc.tensor.matmul_mx(
+                out=acc[:],
+                lhsT=w_codes[:, cols].bitcast(FP8X4),
+                lhsT_scale=w_scales[:, cols],
+                rhs=z_codes[:, part].bitcast(FP8X4),
+                rhs_scale=z_scales[:, part],
+                start=True,
+                stop=True,
+            )
+            return acc
+
+        for part, bank in zip(halves, ["acc_h0", "acc_o0"]):
+            nc.scalar.copy(h2[0][:, part], product(0, part, bank)[:])
+        for m in range(1, blocks):
+            nc.vector.tensor_copy(h2[m][:], product(m, slice(0, S), "acc_o%d" % m)[:])
+
+        ra = [keep.tile([P, W], F32, name="ra%d" % m) for m in range(blocks)]
+        rb = [keep.tile([P, W], F32, name="rb%d" % m) for m in range(blocks)]
+        for m in range(blocks):
+            pa = keep.tile([P, W], F32, name="pa%d" % m)
+            pb = keep.tile([P, W], F32, name="pb%d" % m)
+            nc.scalar.activation(pa[:], h2[m][:].indirect(n3_t[:]), COPY)
+            nc.scalar.activation(pb[:], h2[m][:].indirect(n4_t[:]), COPY)
+            nc.vector.tensor_tensor(ra[m][:], pa[:], pb[:], ALU.add)
+            nc.vector.tensor_tensor(rb[m][:], pa[:], pb[:], ALU.max)
+
+        def put(m):
+            nc.scalar.activation(ub_t[m][:].indirect(n5_t[:]), ra[m][:], COPY)
+            nc.scalar.activation(ub_t[m][:].indirect(n6_t[:]), rb[m][:], COPY)
+
+        def finish(m, part, queue):
+            width = part.stop - part.start
+            far = keep.tile([P, width], F32, name="far%d_%d" % (m, part.start))
+            nc.scalar.activation(far[:], ub_t[m][:].indirect(n7_t[:, part.start // 16 : part.stop // 16]), COPY)
+            res = keep.tile([P, width], F32, name="res%d_%d" % (m, part.start))
+            nc.vector.tensor_tensor(res[:], ub_t[m][:, part], far[:], ALU.subtract)
+            queue.dma_start(out[m * P : (m + 1) * P, part], res[:])
+
+        put(0)
+        for m in range(1, blocks):
+            put(m)
+            finish(m - 1, slice(0, S), nc.sync)
+        finish(blocks - 1, halves[0], nc.sync)
+        finish(blocks - 1, halves[1], nc.scalar)

@@ -39,17 +39,17 @@ def tile_picked_mhhznsendhopcphd_none_p_kernel(
         d_tab = keep.tile([P, G], U32, align_bytes=64)
         x_tab = keep.tile([P, T], U32, align_bytes=64)
         offs_t = load_list("offs_t", offs)
-        nc.sync.dma_start(
+        nc.scalar.dma_start(
             x_bytes[:].bitcast(I32), x_scales[0].bitcast(I32).unsqueeze(1).to_broadcast([16, 8, T // 4])
         )
         hz_t = load_list("hz_t", hz)
-        nc.sync.dma_start(
+        nc.scalar.dma_start(
             d_bytes[:].bitcast(I32), d_scales[0].bitcast(I32).unsqueeze(1).to_broadcast([16, 8, G // 4])
         )
         k1_t = load_list("k1_t", k1)
         k2_t = load_list("k2_t", k2)
-        nc.sync.dma_start(d_tab[:].bitcast(I32), d_words[0].rearrange("p c r -> p (c r)").bitcast(I32))
         nc.sync.dma_start(x_tab[:].bitcast(I32), x_words[0].rearrange("p c r -> p (c r)").bitcast(I32))
+        nc.sync.dma_start(d_tab[:].bitcast(I32), d_words[0].rearrange("p c r -> p (c r)").bitcast(I32))
 
         n1_t = load_list("n1_t", n1)
         n2_t = load_list("n2_t", n2)
@@ -61,41 +61,39 @@ def tile_picked_mhhznsendhopcphd_none_p_kernel(
         gain = [keep.tile([P, 1], F32, name="gain%d" % t) for t in range(SLOTS)]
         gn_rows = gn.rearrange("(b t q) o -> t b q o", t=SLOTS, q=8)
         for t in range(SLOTS):
-            nc.sync.dma_start(gain[t][:], gn_rows[t])
+            nc.gpsimd.dma_start(gain[t][:], gn_rows[t])
 
-        planes = keep.tile([P, 2 * H + 2 * S], U8, align_bytes=64)
-        nc.vector.memset(planes[:].bitcast(I32), 0)
         h_t = [keep.tile([P, S + SPARE], F32, name="h%d" % t) for t in range(SLOTS)]
         ub_t = [keep.tile([P, S + SPARE], F32, name="ub%d" % t) for t in range(SLOTS)]
         for tile in h_t + ub_t:
             nc.vector.memset(tile[:, S:], 0.0)
 
-        picked_bytes = keep.tile([P, 2 * H + 2 * S], U8, align_bytes=64)
-        nc.vector.tensor_copy(picked_bytes[:, 2 * H : 2 * H + S], x_bytes[:].indirect(offs_t[:]))
-        nc.vector.tensor_copy(picked_bytes[:, 2 * H + S :], x_bytes[:].indirect(hz_t[:]))
-        nc.vector.tensor_copy(picked_bytes[:, 0:H], d_bytes[:].indirect(k1_t[:]))
-        nc.vector.tensor_copy(picked_bytes[:, H : 2 * H], d_bytes[:].indirect(k2_t[:]))
-        dealt_bytes = keep.tile([P, 2 * H + 2 * S], U8, tag="staging", align_bytes=64)
-        nc.vector.tensor_copy(dealt_bytes[:, 2 * H :].bitcast(I32), picked_bytes[:, 2 * H :].bitcast(I32))
-        nc.vector.tensor_copy(
-            dealt_bytes[:, : 2 * H].bitcast(I32).rearrange("p (l t b w) -> p l t b w", l=2, t=SLOTS, w=2),
-            picked_bytes[:, : 2 * H].bitcast(I32).rearrange("p (l b t w) -> p l t b w", l=2, t=SLOTS, w=2),
-        )
-        for a in range(4):
-            queue = nc.sync if a % 2 == 0 else nc.scalar
-            queue.dma_start(planes[a:P:32, :].bitcast(I32), dealt_bytes[8 * a : P : 32, :].bitcast(I32))
-
+        picked_bytes = keep.tile([P, 2 * H + 2 * S], U8, tag="staging", align_bytes=64)
+        planes = keep.tile([P, 2 * H + 2 * S], U8, align_bytes=64)
         picked_d = keep.tile([P, 2 * H], U32, align_bytes=64)
         picked_x = [keep.tile([P, S], U32, name="picked_x%d" % l, align_bytes=64) for l in range(2)]
         dealt_d = keep.tile([P, 2 * H], U32, align_bytes=64)
         deal_to = dealt_d[:].rearrange("p (l t b q) -> p l t b q", l=2, t=SLOTS, q=8)
         deal_from = picked_d[:].rearrange("p (l b t q) -> p l t b q", l=2, t=SLOTS, q=8)
 
+        nc.vector.tensor_copy(picked_bytes[:, 2 * H : 2 * H + S], x_bytes[:].indirect(offs_t[:]))
+        nc.vector.tensor_copy(picked_bytes[:, 2 * H + S :], x_bytes[:].indirect(hz_t[:]))
+        nc.vector.tensor_copy(picked_bytes[:, 0:H], d_bytes[:].indirect(k1_t[:]))
+        nc.vector.tensor_copy(planes[:, 2 * H :].bitcast(I32), picked_bytes[:, 2 * H :].bitcast(I32))
+        nc.vector.tensor_copy(picked_bytes[:, H : 2 * H], d_bytes[:].indirect(k2_t[:]))
+        nc.vector.tensor_copy(picked_x[0][:], x_tab[:].indirect(offs_t[:]))
+        nc.vector.tensor_copy(
+            planes[:, : 2 * H].bitcast(I32).rearrange("p (l t b w) -> p l t b w", l=2, t=SLOTS, w=2),
+            picked_bytes[:, : 2 * H].bitcast(I32).rearrange("p (l b t w) -> p l t b w", l=2, t=SLOTS, w=2),
+        )
+        for a in range(1, 4):
+            nc.sync.dma_start(planes[a:P:32, :].bitcast(I32), planes[8 * a : P : 32, :].bitcast(I32))
+
         nc.vector.tensor_copy(picked_d[:, :H], d_tab[:].indirect(k1_t[:]))
         nc.vector.tensor_copy(picked_d[:, H:], d_tab[:].indirect(k2_t[:]))
-        nc.vector.tensor_copy(picked_x[0][:], x_tab[:].indirect(offs_t[:]))
-        nc.vector.tensor_copy(deal_to[:, :, 0], deal_from[:, :, 0])
+        nc.vector.tensor_copy(deal_to[:, 0, 0], deal_from[:, 0, 0])
         nc.vector.tensor_copy(picked_x[1][:], x_tab[:].indirect(hz_t[:]))
+        nc.vector.tensor_copy(deal_to[:, 1, 0], deal_from[:, 1, 0])
         nc.vector.tensor_copy(deal_to[:, :, 1:], deal_from[:, :, 1:])
 
         w_raw = keep.tile([P, SLOTS, N], F32, tag="staging", align_bytes=64)
@@ -104,7 +102,6 @@ def tile_picked_mhhznsendhopcphd_none_p_kernel(
             nc.sync.dma_start(w_raw[:, t, :], w_rows[t])
 
         halves = [slice(0, S // 2), slice(S // 2, S)]
-        z_bf = keep.tile([P, S, SLOTS], BF16, align_bytes=64)
         w_codes = keep.tile([P, N], U32, align_bytes=64)
         w_scales = keep.tile([P, N], U8, align_bytes=64)
 
@@ -131,22 +128,23 @@ def tile_picked_mhhznsendhopcphd_none_p_kernel(
             nc.scalar.activation(hopped[t][:], h_t[t][:].indirect(n1_t[:]), COPY)
             nc.vector.tensor_tensor(st[t][:], h_t[t][:, :S], hopped[t][:], ALU.max)
 
+        w_bf = keep.tile([P, N, SLOTS], BF16, tag="rounded", align_bytes=64)
+        for m in range(N // P):
+            cols = slice(m * P, (m + 1) * P)
+            nc.vector.tensor_copy(
+                w_bf[:, cols, :].rearrange("p (c i) t -> p c t i", i=4),
+                w_raw[:, :, cols].rearrange("p t (c i) -> p c t i", i=4),
+            )
+        nc.vector.quantize_mx(
+            out=w_codes[:].bitcast(FP8X4), scales=w_scales[:], in_=w_bf[:].rearrange("p c t -> p (c t)")
+        )
+
+        z_bf = keep.tile([P, S, SLOTS], BF16, tag="rounded", align_bytes=64)
         for t in range(SLOTS):
             ds = keep.tile([P, SCATTER_COLS], F32, name="ds%d" % t)
             nc.scalar.activation(ds[:].indirect(n2_t[:]), st[t][:], COPY)
             gained_h = keep.tile([P, S], F32, name="gained_h%d" % t)
             nc.vector.tensor_scalar(gained_h[:], h_t[t][:, :S], gain[t][:], None, ALU.mult)
-            cols = slice(t * P, (t + 1) * P)
-            w_bf = keep.tile([P, P, SLOTS], BF16, name="w_bf%d" % t, align_bytes=64)
-            nc.vector.tensor_copy(
-                w_bf[:].rearrange("p (c i) t -> p c t i", i=4),
-                w_raw[:, :, cols].rearrange("p t (c i) -> p c t i", i=4),
-            )
-            nc.vector.quantize_mx(
-                out=w_codes[:, cols].bitcast(FP8X4),
-                scales=w_scales[:, cols],
-                in_=w_bf[:].rearrange("p c t -> p (c t)"),
-            )
             for part in halves if t == SLOTS - 1 else [slice(0, S)]:
                 nc.vector.scalar_tensor_tensor(
                     z_bf[:, part, t], ds[:, part], gain[t][:], gained_h[:, part], ALU.mult, ALU.subtract
@@ -193,8 +191,9 @@ def tile_picked_mhhznsendhopcphd_none_p_kernel(
             nc.vector.tensor_tensor(ra[m][:], pa[:], pb[:], ALU.add)
             nc.vector.tensor_tensor(rb[m][:], pa[:], pb[:], ALU.max)
 
-        def put(m):
+        for m in range(blocks):
             nc.scalar.activation(ub_t[m][:].indirect(n5_t[:]), ra[m][:], COPY)
+        for m in range(blocks):
             nc.scalar.activation(ub_t[m][:].indirect(n6_t[:]), rb[m][:], COPY)
 
         def finish(m, part, queue):
@@ -205,9 +204,7 @@ def tile_picked_mhhznsendhopcphd_none_p_kernel(
             nc.vector.tensor_tensor(res[:], ub_t[m][:, part], far[:], ALU.subtract)
             queue.dma_start(out[m * P : (m + 1) * P, part], res[:])
 
-        put(0)
-        for m in range(1, blocks):
-            put(m)
-            finish(m - 1, slice(0, S), nc.sync)
+        for m in range(blocks - 1):
+            finish(m, slice(0, S), nc.sync)
         finish(blocks - 1, halves[0], nc.sync)
         finish(blocks - 1, halves[1], nc.scalar)

@@ -58,10 +58,6 @@ def tile_picked_mhhznsendhopcphd_none_p_kernel(
         n5_t = load_list("n5_t", n5)
         n6_t = load_list("n6_t", n6)
         n7_t = load_list("n7_t", n7)
-        gain = [keep.tile([P, 1], F32, name="gain%d" % t) for t in range(SLOTS)]
-        gn_rows = gn.rearrange("(b t q) o -> t b q o", t=SLOTS, q=8)
-        for t in range(SLOTS):
-            nc.gpsimd.dma_start(gain[t][:], gn_rows[t])
 
         h_t = [keep.tile([P, S + SPARE], F32, name="h%d" % t) for t in range(SLOTS)]
         ub_t = [keep.tile([P, S + SPARE], F32, name="ub%d" % t) for t in range(SLOTS)]
@@ -96,10 +92,14 @@ def tile_picked_mhhznsendhopcphd_none_p_kernel(
         nc.vector.tensor_copy(deal_to[:, 1, 0], deal_from[:, 1, 0])
         nc.vector.tensor_copy(deal_to[:, :, 1:], deal_from[:, :, 1:])
 
-        w_raw = keep.tile([P, SLOTS, N], F32, tag="staging", align_bytes=64)
+        w_raw = keep.tile([P, SLOTS, N + 8], F32, tag="staging", align_bytes=64)
         w_rows = w1.rearrange("(b t q) n -> t b q n", t=SLOTS, q=8)
+        gn_rows = gn.rearrange("(b t q) o -> t b q o", t=SLOTS, q=8)
+        gain = [w_raw[:, t, N : N + 1] for t in range(SLOTS)]
         for t in range(SLOTS):
-            nc.sync.dma_start(w_raw[:, t, :], w_rows[t])
+            nc.sync.dma_start(w_raw[:, t, :N], w_rows[t])
+        for t in range(SLOTS):
+            nc.sync.dma_start(gain[t], gn_rows[t])
 
         halves = [slice(0, S // 2), slice(S // 2, S)]
         w_codes = keep.tile([P, N], U32, align_bytes=64)
@@ -139,16 +139,22 @@ def tile_picked_mhhznsendhopcphd_none_p_kernel(
             out=w_codes[:].bitcast(FP8X4), scales=w_scales[:], in_=w_bf[:].rearrange("p c t -> p (c t)")
         )
 
-        z_bf = keep.tile([P, S, SLOTS], BF16, tag="rounded", align_bytes=64)
+        z_all = keep.tile([P, (2 * SLOTS - 1) * S], BF16, tag="rounded", align_bytes=64)
+        z_bf = z_all[:, : SLOTS * S].rearrange("p (j t) -> p j t", t=SLOTS)
+        z_rows = z_all[:, SLOTS * S :].rearrange("p (t j) -> p t j", j=S)
         for t in range(SLOTS):
             ds = keep.tile([P, SCATTER_COLS], F32, name="ds%d" % t)
             nc.scalar.activation(ds[:].indirect(n2_t[:]), st[t][:], COPY)
             gained_h = keep.tile([P, S], F32, name="gained_h%d" % t)
-            nc.vector.tensor_scalar(gained_h[:], h_t[t][:, :S], gain[t][:], None, ALU.mult)
-            for part in halves if t == SLOTS - 1 else [slice(0, S)]:
-                nc.vector.scalar_tensor_tensor(
-                    z_bf[:, part, t], ds[:, part], gain[t][:], gained_h[:, part], ALU.mult, ALU.subtract
-                )
+            nc.vector.tensor_scalar(gained_h[:], h_t[t][:, :S], gain[t], None, ALU.mult)
+            if t < SLOTS - 1:
+                nc.vector.scalar_tensor_tensor(z_rows[:, t, :], ds[:, :S], gain[t], gained_h[:], ALU.mult, ALU.subtract)
+            else:
+                nc.vector.tensor_copy(z_bf[:, :, :t], z_rows.rearrange("p t j -> p j t"))
+                for part in halves:
+                    nc.vector.scalar_tensor_tensor(
+                        z_bf[:, part, t], ds[:, part], gain[t], gained_h[:, part], ALU.mult, ALU.subtract
+                    )
 
         z_codes = keep.tile([P, S], U32, align_bytes=64)
         z_scales = keep.tile([P, S], U8, align_bytes=64)
@@ -156,7 +162,7 @@ def tile_picked_mhhznsendhopcphd_none_p_kernel(
             nc.vector.quantize_mx(
                 out=z_codes[:, part].bitcast(FP8X4),
                 scales=z_scales[:, part],
-                in_=z_bf[:, part, :].rearrange("p j t -> p (j t)"),
+                in_=z_all[:, SLOTS * part.start : SLOTS * part.stop],
             )
 
         blocks = N // P
@@ -206,5 +212,5 @@ def tile_picked_mhhznsendhopcphd_none_p_kernel(
 
         for m in range(blocks - 1):
             finish(m, slice(0, S), nc.sync)
-        finish(blocks - 1, halves[0], nc.sync)
-        finish(blocks - 1, halves[1], nc.scalar)
+        finish(blocks - 1, slice(0, 192), nc.sync)
+        finish(blocks - 1, slice(192, S), nc.scalar)

from contextlib import ExitStack

import concourse.mybir as mybir

K, T, S, N, G, H, W = 512, 1024, 256, 512, 2048, 512, 128
FLOPS = 2 * (2 * K * H * S + H * N * S)

F32 = mybir.dt.float32
BF16 = mybir.dt.bfloat16
I32 = mybir.dt.int32
U32 = mybir.dt.uint32
U16 = mybir.dt.uint16
U8 = mybir.dt.uint8
FP8X4 = mybir.dt.float8_e4m3fn_x4
ALU = mybir.AluOpType
COPY = mybir.ActivationFunctionType.Copy

P = 128
SLOTS = 4
SPARE = 8
SCATTER_COLS = 352


def tile_picked_mhhznsendhopcphd_none_p_kernel(
    tc, x_words, x_scales, d_words, d_scales, gn, w1, offs, k1, hz, k2, n1, n2, n3, n4, n5, n6, n7, out
):
    nc = tc.nc
    with ExitStack() as ctx:
        keep = ctx.enter_context(tc.tile_pool(name="keep", bufs=1))
        psum = ctx.enter_context(tc.psum_pool(name="psum", bufs=1))

        def load_list(name, src):
            tile = keep.tile(list(src.shape), U16, name=name)
            nc.sync.dma_start(tile[:], src)
            return tile

        d_bytes = keep.tile([P, G], U8, align_bytes=64)
        x_bytes = keep.tile([P, T], U8, align_bytes=64)
        d_tab = keep.tile([P, G], U32, align_bytes=64)
        x_tab = keep.tile([P, T], U32, align_bytes=64)
        offs_t = load_list("offs_t", offs)
        nc.scalar.dma_start(
            x_bytes[:].bitcast(I32), x_scales[0].bitcast(I32).unsqueeze(1).to_broadcast([16, 8, T // 4])
        )
        hz_t = load_list("hz_t", hz)
        nc.scalar.dma_start(
            d_bytes[:].bitcast(I32), d_scales[0].bitcast(I32).unsqueeze(1).to_broadcast([16, 8, G // 4])
        )
        k1_t = load_list("k1_t", k1)
        k2_t = load_list("k2_t", k2)
        nc.sync.dma_start(x_tab[:].bitcast(I32), x_words[0].rearrange("p c r -> p (c r)").bitcast(I32))
        nc.sync.dma_start(d_tab[:].bitcast(I32), d_words[0].rearrange("p c r -> p (c r)").bitcast(I32))

        n1_t = load_list("n1_t", n1)
        n2_t = load_list("n2_t", n2)
        n3_t = load_list("n3_t", n3)
        n4_t = load_list("n4_t", n4)
        n5_t = load_list("n5_t", n5)
        n6_t = load_list("n6_t", n6)
        n7_t = load_list("n7_t", n7)

        h_t = [keep.tile([P, S + SPARE], F32, name="h%d" % t) for t in range(SLOTS)]
        ub_t = [keep.tile([P, S + SPARE], F32, name="ub%d" % t) for t in range(SLOTS)]
        for tile in h_t + ub_t:
            nc.vector.memset(tile[:, S:], 0.0)

        picked_bytes = keep.tile([P, 2 * H + 2 * S], U8, tag="staging", align_bytes=64)
        planes = keep.tile([P, 2 * H + 2 * S], U8, align_bytes=64)
        picked_d = keep.tile([P, 2 * H], U32, align_bytes=64)
        picked_x = [keep.tile([P, S], U32, name="picked_x%d" % l, align_bytes=64) for l in range(2)]
        dealt_d = keep.tile([P, 2 * H], U32, align_bytes=64)
        deal_to = dealt_d[:].rearrange("p (l t b q) -> p l t b q", l=2, t=SLOTS, q=8)
        deal_from = picked_d[:].rearrange("p (l b t q) -> p l t b q", l=2, t=SLOTS, q=8)

        nc.vector.tensor_copy(picked_bytes[:, 2 * H : 2 * H + S], x_bytes[:].indirect(offs_t[:]))
        nc.vector.tensor_copy(picked_bytes[:, 2 * H + S :], x_bytes[:].indirect(hz_t[:]))
        nc.vector.tensor_copy(picked_bytes[:, 0:H], d_bytes[:].indirect(k1_t[:]))
        nc.vector.tensor_copy(planes[:, 2 * H :].bitcast(I32), picked_bytes[:, 2 * H :].bitcast(I32))
        nc.vector.tensor_copy(picked_bytes[:, H : 2 * H], d_bytes[:].indirect(k2_t[:]))
        nc.vector.tensor_copy(picked_x[0][:], x_tab[:].indirect(offs_t[:]))
        nc.vector.tensor_copy(
            planes[:, : 2 * H].bitcast(I32).rearrange("p (l t b w) -> p l t b w", l=2, t=SLOTS, w=2),
            picked_bytes[:, : 2 * H].bitcast(I32).rearrange("p (l b t w) -> p l t b w", l=2, t=SLOTS, w=2),
        )
        for a in range(1, 4):
            nc.sync.dma_start(planes[a:P:32, :].bitcast(I32), planes[8 * a : P : 32, :].bitcast(I32))

        nc.vector.tensor_copy(picked_d[:, :H], d_tab[:].indirect(k1_t[:]))
        nc.vector.tensor_copy(picked_d[:, H:], d_tab[:].indirect(k2_t[:]))
        nc.vector.tensor_copy(deal_to[:, 0, 0], deal_from[:, 0, 0])
        nc.vector.tensor_copy(picked_x[1][:], x_tab[:].indirect(hz_t[:]))
        nc.vector.tensor_copy(deal_to[:, 1, 0], deal_from[:, 1, 0])
        nc.vector.tensor_copy(deal_to[:, :, 1:], deal_from[:, :, 1:])

        w_raw = keep.tile([P, SLOTS, N + 8], F32, tag="staging", align_bytes=64)
        w_rows = w1.rearrange("(b t q) n -> t b q n", t=SLOTS, q=8)
        gn_rows = gn.rearrange("(b t q) o -> t b q o", t=SLOTS, q=8)
        gain = [w_raw[:, t, N : N + 1] for t in range(SLOTS)]
        for t in range(SLOTS):
            nc.sync.dma_start(w_raw[:, t, :N], w_rows[t])
        for t in range(SLOTS):
            nc.sync.dma_start(gain[t], gn_rows[t])

        halves = [slice(0, S // 2), slice(S // 2, S)]
        w_codes = keep.tile([P, N], U32, align_bytes=64)
        w_scales = keep.tile([P, N], U8, align_bytes=64)

        acc_h = [psum.tile([P, S], F32, name="acc_h%d" % t) for t in range(SLOTS)]
        for t in range(SLOTS):
            for l in range(2):
                cols = slice(l * H + t * P, l * H + (t + 1) * P)
                nc.tensor.matmul_mx(
                    out=acc_h[t][:],
                    lhsT=dealt_d[:, cols].bitcast(FP8X4),
                    lhsT_scale=planes[:, cols],
                    rhs=picked_x[l][:].bitcast(FP8X4),
                    rhs_scale=planes[:, 2 * H + l * S : 2 * H + (l + 1) * S],
                    start=(l == 0),
                    stop=(l == 1),
                )

        nc.scalar.activation(h_t[0][:, :S], acc_h[0][:], COPY, scale=0.0625)
        for t in range(1, SLOTS):
            nc.vector.tensor_scalar(h_t[t][:, :S], acc_h[t][:], 0.0625, None, ALU.mult)
        hopped = [keep.tile([P, S], F32, name="hopped%d" % t) for t in range(SLOTS)]
        st = [keep.tile([P, S], F32, name="st%d" % t) for t in range(SLOTS)]
        for t in range(SLOTS):
            nc.scalar.activation(hopped[t][:], h_t[t][:].indirect(n1_t[:]), COPY)
            nc.vector.tensor_tensor(st[t][:], h_t[t][:, :S], hopped[t][:], ALU.max)

        w_bf = keep.tile([P, N, SLOTS], BF16, tag="rounded", align_bytes=64)
        for m in range(N // P):
            cols = slice(m * P, (m + 1) * P)
            nc.vector.tensor_copy(
                w_bf[:, cols, :].rearrange("p (c i) t -> p c t i", i=4),
                w_raw[:, :, cols].rearrange("p t (c i) -> p c t i", i=4),
            )
        nc.vector.quantize_mx(
            out=w_codes[:].bitcast(FP8X4), scales=w_scales[:], in_=w_bf[:].rearrange("p c t -> p (c t)")
        )

        z_all = keep.tile([P, (2 * SLOTS - 1) * S], BF16, tag="rounded", align_bytes=64)
        z_bf = z_all[:, : SLOTS * S].rearrange("p (j t) -> p j t", t=SLOTS)
        z_rows = z_all[:, SLOTS * S :].rearrange("p (t j) -> p t j", j=S)
        for t in range(SLOTS):
            ds = keep.tile([P, SCATTER_COLS], F32, name="ds%d" % t)
            nc.scalar.activation(ds[:].indirect(n2_t[:]), st[t][:], COPY)
            gained_h = keep.tile([P, S], F32, name="gained_h%d" % t)
            nc.vector.tensor_scalar(gained_h[:], h_t[t][:, :S], gain[t], None, ALU.mult)
            if t < SLOTS - 1:
                nc.vector.scalar_tensor_tensor(z_rows[:, t, :], ds[:, :S], gain[t], gained_h[:], ALU.mult, ALU.subtract)
            else:
                nc.vector.tensor_copy(z_bf[:, :, :t], z_rows.rearrange("p t j -> p j t"))
                for part in halves:
                    nc.vector.scalar_tensor_tensor(
                        z_bf[:, part, t], ds[:, part], gain[t], gained_h[:, part], ALU.mult, ALU.subtract
                    )

        z_codes = keep.tile([P, S], U32, align_bytes=64)
        z_scales = keep.tile([P, S], U8, align_bytes=64)
        for part in halves:
            nc.vector.quantize_mx(
                out=z_codes[:, part].bitcast(FP8X4),
                scales=z_scales[:, part],
                in_=z_all[:, SLOTS * part.start : SLOTS * part.stop],
            )

        blocks = N // P
        h2 = [keep.tile([P, S], F32, name="h2_%d" % m) for m in range(blocks)]

        def product(m, part, bank):
            cols = slice(m * P, (m + 1) * P)
            acc = psum.tile([P, part.stop - part.start], F32, name=bank)
            nc.tensor.matmul_mx(
                out=acc[:],
                lhsT=w_codes[:, cols].bitcast(FP8X4),
                lhsT_scale=w_scales[:, cols],
                rhs=z_codes[:, part].bitcast(FP8X4),
                rhs_scale=z_scales[:, part],
                start=True,
                stop=True,
            )
            return acc

        for part, bank in zip(halves, ["acc_h0", "acc_o0"]):
            nc.scalar.copy(h2[0][:, part], product(0, part, bank)[:])
        for m in range(1, blocks):
            nc.vector.tensor_copy(h2[m][:], product(m, slice(0, S), "acc_o%d" % m)[:])

        ra = [keep.tile([P, W], F32, name="ra%d" % m) for m in range(blocks)]
        rb = [keep.tile([P, W], F32, name="rb%d" % m) for m in range(blocks)]
        for m in range(blocks):
            pa = keep.tile([P, W], F32, name="pa%d" % m)
            pb = keep.tile([P, W], F32, name="pb%d" % m)
            nc.scalar.activation(pa[:], h2[m][:].indirect(n3_t[:]), COPY)
            nc.scalar.activation(pb[:], h2[m][:].indirect(n4_t[:]), COPY)
            nc.vector.tensor_tensor(ra[m][:], pa[:], pb[:], ALU.add)
            nc.vector.tensor_tensor(rb[m][:], pa[:], pb[:], ALU.max)

        for m in range(blocks):
            nc.scalar.activation(ub_t[m][:].indirect(n5_t[:]), ra[m][:], COPY)
        for m in range(blocks):
            nc.scalar.activation(ub_t[m][:].indirect(n6_t[:]), rb[m][:], COPY)

        def finish(m, part, queue):
            width = part.stop - part.start
            far = keep.tile([P, width], F32, name="far%d_%d" % (m, part.start))
            nc.scalar.activation(far[:], ub_t[m][:].indirect(n7_t[:, part.start // 16 : part.stop // 16]), COPY)
            res = keep.tile([P, width], F32, name="res%d_%d" % (m, part.start))
            nc.vector.tensor_tensor(res[:], ub_t[m][:, part], far[:], ALU.subtract)
            queue.dma_start(out[m * P : (m + 1) * P, part], res[:])

        for m in range(blocks - 1):
            finish(m, slice(0, S), nc.sync)
        finish(blocks - 1, slice(0, 192), nc.sync)
        finish(blocks - 1, slice(192, S), nc.scalar)
